import numpy as np
import ml_dtypes


def mxq(x, axis, fmt="e4m3"):
    dtype, down = {"e4m3": (ml_dtypes.float8_e4m3fn, 7), "e5m2": (ml_dtypes.float8_e5m2, 14)}[fmt]
    v = np.moveaxis(np.asarray(x, np.float32).astype(ml_dtypes.bfloat16).astype(np.float64), axis, -1)
    blocks = v.reshape(v.shape[:-1] + (-1, 32))
    amax = np.abs(blocks).max(-1, keepdims=True)
    byte = np.maximum(np.where(amax > 0, np.frexp(amax)[1] - 1 + 127, 0) - down, 1)
    scale = np.exp2(byte - 127.0)
    codes = (blocks / scale).astype(np.float32).astype(dtype).astype(np.float64)
    return np.moveaxis((codes * scale).reshape(v.shape), -1, axis)


WIDE = False


def mx_kscale(k):
    if not WIDE:
        return np.ones(k)
    levels = np.array([10, -10, 5, -5, 0])
    if k % 512:
        return np.exp2(np.random.permutation(np.resize(levels, k // 32))).repeat(32)
    a = np.empty((k // 512, 16))
    for p in range(k // 512):
        a[p, :8] = np.random.permutation(np.resize(levels, 8))
        for g in range(8):
            far = levels[np.abs(levels - a[p, g]) >= 10]
            a[p, g + 8] = far[np.random.randint(len(far))]
    return np.exp2(a.ravel()).repeat(32)


BF16 = ml_dtypes.bfloat16


def bf(x):
    return np.asarray(x, np.float32).astype(BF16)


def f64(x):
    return np.asarray(x).astype(np.float64)


B, D, X = 6144, 512, 512


def _euler(state, z):
    return state + 0.5 * (np.tanh(z) - 0.5 * state)


def draw0():
    s, t = mx_kscale(X), mx_kscale(D)
    return {"h": bf(np.random.standard_normal((B, D)) * 0.5),
            "x": bf(np.random.standard_normal((B, X)) * s),
            "w": bf(np.random.standard_normal((D, D)) * np.sqrt(2.0 / D)),
            "win": bf(np.random.standard_normal((X, D)) / np.sqrt(X) / s[:, None]),
            "b": bf(np.random.standard_normal(D) * 0.3),
            "p": bf((1.0 + 0.25 * np.random.standard_normal(D)) * t),
            "r": bf((1.0 + 0.25 * np.random.standard_normal(D)) / t)}


def core(h, x, w, win, b, p, r):
    h, w, b, p, r = f64(h), f64(w), f64(b), f64(p), f64(r)
    a = mxq(r[:, None] * (w - w.T), 0, "e4m3")
    c = (mxq(f64(x), 1, "e4m3") @ mxq(f64(win), 0, "e4m3")) + b[None, :]
    z1 = (mxq(h * p[None, :], 1, "e4m3") @ a) + c
    u1 = _euler(h, z1)
    z2 = (mxq(u1 * p[None, :], 1, "e4m3") @ a) + c
    return 0.5 * h + 0.5 * _euler(u1, z2)


def e4m3fn_bytes(y):
    return np.clip(np.asarray(y, np.float64), -448.0, 448.0).astype(np.float32).astype(ml_dtypes.float8_e4m3fn).view(np.uint8)


def e4m3fn_values(b):
    return np.asarray(b, np.uint8).view(ml_dtypes.float8_e4m3fn).astype(np.float64)


def setup_inputs():
    d = draw0()
    x0 = np.asarray(d['x']).astype(np.float64)
    s = (np.max(np.abs(x0), axis=(0,), keepdims=True) / 448.0).astype(np.float32)
    out = {}
    for k, v in d.items():
        if k == 'x':
            out['x_bytes'] = e4m3fn_bytes(x0 / s.astype(np.float64))
            out['x_scale'] = s
        else:
            out[k] = v
    return out


def reference(h, x_bytes, x_scale, w, win, b, p, r):
    return core(h, e4m3fn_values(x_bytes) * x_scale.astype(np.float64), w, win, b, p, r)

@@ -1,0 +1,255 @@
+from contextlib import ExitStack
+
+import concourse.mybir as mybir
+from concourse.masks import make_identity
+
+F32 = mybir.dt.float32
+BF16 = mybir.dt.bfloat16
+U32 = mybir.dt.uint32
+U8 = mybir.dt.uint8
+FP8 = mybir.dt.float8_e4m3fn
+FP8X4 = mybir.dt.float8_e4m3fn_x4
+ACT = mybir.ActivationFunctionType
+ALU = mybir.AluOpType
+
+B, D, X = 6144, 512, 512
+P = 128
+N = 256
+Q = N // P
+T = 4
+NG = B // N
+
+FLOPS = 3 * 2 * B * D * D
+
+
+def tile_antisymmetricssprk2step_t_kernel(tc, h, x_bytes, x_scale, w, win, b, p, r, out):
+    nc = tc.nc
+    h_g = h.rearrange("(g p q) d -> g p q d", p=P, q=Q)
+    x_g = x_bytes.rearrange("(g p q) d -> g p q d", p=P, q=Q)
+    o_g = out.rearrange("(g p q) d -> g p q d", p=P, q=Q)
+
+    with ExitStack() as ctx:
+        keep = ctx.enter_context(tc.tile_pool(name="keep", bufs=1))
+        sb = ctx.enter_context(tc.tile_pool(name="sb", bufs=2))
+        ps = ctx.enter_context(tc.psum_pool(name="ps", bufs=1))
+        ctx.enter_context(tc.manual_schedule())
+
+        def st(nm, shape, dt, bufs):
+            return sb.tile(shape, dt, name=nm, tag=nm, bufs=bufs, align_bytes=64)
+
+        def kt(nm, shape, dt):
+            return keep.tile(shape, dt, name=nm, tag=nm, align_bytes=64)
+
+        ht, xt, xs, hp, xg, hq, xq, h1, t1, xx, up, uq, t2, z1, z2, xb, xp, hps = ({} for j in range(18))
+
+        def load(g):
+            xb[g] = st("xb", [P, Q, X], U8, 5)
+            nc.sync.dma_start(out=xb[g][:], in_=x_g[g])
+            ht[g] = st("ht", [P, Q, D], BF16, 9)
+            nc.sync.dma_start(out=ht[g][:], in_=h_g[g])
+
+        ident = kt("ident", [P, P], F32)
+        make_identity(nc, ident[:])
+        ident_b = kt("ident_b", [P, P], BF16)
+        make_identity(nc, ident_b[:])
+        warm = kt("warm", [P, 1], F32)
+        nc.vector.memset(warm[:], 0.0)
+        nc.scalar.activation(out=warm[:], in_=warm[:], func=ACT.Tanh)
+
+        sc = kt("sc", [P, Q, X], F32)
+        nc.scalar.dma_start(out=sc[:, 0, :], in_=x_scale.rearrange("o k -> (o k)").partition_broadcast(P))
+        pb = kt("pb", [P, 2, 2], BF16)
+        rb = kt("rb", [P, T], BF16)
+        bb = kt("bb", [P, T], BF16)
+        nc.scalar.dma_start(out=rb[:], in_=r.rearrange("(p t) -> p t", t=T))
+        nc.scalar.dma_start(out=pb[:], in_=p.rearrange("(p u e) -> p u e", u=2, e=2))
+        nc.scalar.dma_start(out=bb[:], in_=b.rearrange("(p t) -> p t", t=T))
+
+        w_raw = kt("w_raw", [P, T, D], BF16)
+        win_raw = kt("win_raw", [P, T, D], BF16)
+        xb[0] = st("xb", [P, Q, X], U8, 5)
+        nc.sync.dma_start(out=xb[0][:], in_=x_g[0])
+        nc.sync.dma_start(out=w_raw[:], in_=w.rearrange("(p j) c -> p j c", j=T))
+        ht[0] = st("ht", [P, Q, D], BF16, 9)
+        nc.sync.dma_start(out=ht[0][:], in_=h_g[0])
+        nc.sync.dma_start(out=win_raw[:], in_=win.rearrange("(p j) c -> p j c", j=T))
+        for g in range(1, 4):
+            load(g)
+
+        nc.scalar.copy(out=sc[:, 1, :], in_=sc[:, 0, :])
+        two_b = kt("two_b", [P, P], BF16)
+        nc.vector.tensor_scalar(out=two_b[:], in0=ident_b[:], scalar1=2.0, scalar2=None, op0=ALU.mult)
+        p23 = kt("p23", [P, T], F32)
+        nc.vector.tensor_scalar(out=p23[:], in0=pb[:].rearrange("p u e -> p (u e)"), scalar1=2.0 / 3.0, scalar2=None, op0=ALU.mult)
+
+        def widen(g):
+            xs[g] = st("xs", [P, Q, X], BF16, 3)
+            nc.vector.tensor_tensor(
+                out=xs[g][:].rearrange("p q k -> p (q k)"),
+                in0=xb[g][:].bitcast(FP8).rearrange("p q k -> p (q k)"),
+                in1=sc[:].rearrange("p q k -> p (q k)"),
+                op=ALU.mult,
+            )
+
+        widen(0)
+
+        wdiff = kt("wdiff", [P, T, D], F32)
+        a_il = kt("a_il", [P, D, T], BF16)
+        for half in range(2):
+            wt = ps.tile([P, 2, T, P], BF16, name="wt", tag="o%d" % half)
+            for jj in range(2):
+                j = 2 * half + jj
+                for t in range(T):
+                    nc.tensor.transpose(wt[:, jj, t, :], w_raw[:, t, j::T], ident_b[:])
+            for jj in range(2):
+                j = 2 * half + jj
+                nc.vector.tensor_tensor(
+                    out=wdiff[:, j, :].rearrange("p (t m) -> p t m", t=T),
+                    in0=w_raw[:, j, :].rearrange("p (m t) -> p t m", t=T),
+                    in1=wt[:, jj],
+                    op=ALU.subtract,
+                )
+        nc.vector.tensor_tensor(
+            out=a_il[:],
+            in0=wdiff[:].rearrange("p j s -> p s j"),
+            in1=rb[:].unsqueeze(1).to_broadcast([P, D, T]),
+            op=ALU.mult,
+        )
+        win_il = kt("win_il", [P, D, T], BF16)
+        for t in range(T):
+            nc.scalar.copy(
+                out=win_il[:, t * P : (t + 1) * P, :],
+                in_=win_raw[:].rearrange("p j (m t) -> p t m j", t=T)[:, t],
+            )
+        aq, asc = kt("aq", [P, D], U32), kt("asc", [P, D], U8)
+        wq, wsc = kt("wq", [P, D], U32), kt("wsc", [P, D], U8)
+
+        def quant(src, codes, scales):
+            nc.vector.quantize_mx(out=codes[:].bitcast(FP8X4), scales=scales[:], in_=src[:].rearrange("p n t -> p (n t)"))
+
+        def turn(tag, src, g):
+            words = src[g][:].bitcast(F32)
+            bank = ps.tile([P, 2, N], F32, name=tag, tag=tag)
+            for q in range(Q):
+                for u in range(2):
+                    nc.tensor.transpose(bank[:, u, q * P : (q + 1) * P], words[:, q, u::2], ident[:])
+            return bank
+
+        def mx(z, g, second):
+            z[g] = []
+            for half in range(2):
+                bank = ps.tile([P, 2, N], F32, name="z%d%d" % (second, half), tag="z%d%d" % (second, half))
+                for tt in range(2):
+                    t = 2 * half + tt
+                    cols = slice(t * P, (t + 1) * P)
+                    m = (uq if second else hq)[g]
+                    for lc, ls, rc, rs, first in ((wq, wsc, xq[g][0], xq[g][1], True), (aq, asc, m[0], m[1], False)):
+                        nc.tensor.matmul_mx(
+                            out=bank[:, tt, :],
+                            lhsT=lc[:, cols].bitcast(FP8X4),
+                            lhsT_scale=ls[:, cols],
+                            rhs=rc[:].bitcast(FP8X4),
+                            rhs_scale=rs[:],
+                            start=first,
+                            stop=not first,
+                        )
+                z[g].append(bank)
+
+        def tanh(z, dst, nm, g):
+            dst[g] = st(nm, [P, T, N], F32, 3)
+            for t in range(T):
+                nc.scalar.activation(out=dst[g][:, t, :], in_=z[g][t // 2][:, t % 2, :], func=ACT.Tanh, bias=bb[:, t : t + 1])
+
+        def ok(g):
+            return 0 <= g < NG
+
+        for i in range(-2, NG + 2):
+            if ok(i + 4) and i + 4 >= 4:
+                load(i + 4)
+            g = i + 1
+            if ok(g):
+                hps[g] = turn("hps", ht, g)
+                xp[g] = turn("xp", xs, g)
+            g = i - 2
+            if ok(g):
+                tanh(z2, t2, "t2", g)
+            g = i - 1
+            if ok(g):
+                xx[g] = st("xx", [P, T, N], F32, 3)
+                nc.vector.scalar_tensor_tensor(out=xx[g][:], in0=t1[g][:], scalar=0.75, in1=h1[g][:], op0=ALU.mult, op1=ALU.add)
+            g = i + 1
+            if ok(g):
+                pairs = hps[g][:].bitcast(BF16).rearrange("p u (n e) -> p u n e", e=2)
+                hp[g] = st("hp", [P, N, T], BF16, 2)
+                nc.vector.tensor_tensor(
+                    out=hp[g][:].rearrange("p n (u e) -> p n u e", e=2),
+                    in0=pairs.rearrange("p u n e -> p n u e"),
+                    in1=pb[:].unsqueeze(1).to_broadcast([P, N, 2, 2]),
+                    op=ALU.mult,
+                )
+                xg[g] = st("xg", [P, N, T], BF16, 2)
+                nc.scalar.copy(out=xg[g][:].bitcast(F32), in_=xp[g][:].rearrange("p u n -> p n u"))
+                h1[g] = st("h1", [P, T, N], F32, 4)
+                nc.scalar.activation(
+                    out=h1[g][:].rearrange("p (u e) n -> p u e n", e=2),
+                    in_=pairs.rearrange("p u n e -> p u e n"),
+                    func=ACT.Copy,
+                    scale=1.125,
+                )
+            g = i - 2
+            banks = []
+            if ok(g):
+                for q in range(Q):
+                    bank = ps.tile([P, T, P], F32, name="o%d" % q, tag="o%d" % q)
+                    nc.tensor.matmul(bank[:], two_b[:], ht[g][:, q, :].rearrange("p (m t) -> p t m", t=T), start=True, stop=False)
+                    for src in (xx, t2):
+                        for t in range(T):
+                            nc.tensor.matmul(
+                                bank[:, t, :], src[g][:, t, q * P : (q + 1) * P], ident[:],
+                                start=False, stop=(src is t2 and t == T - 1), is_transpose=True,
+                            )
+                    banks.append(bank)
+            if i == -1:
+                quant(a_il, aq, asc)
+                quant(win_il, wq, wsc)
+            g = i - 1
+            if ok(g):
+                up[g] = st("up", [P, N, T], BF16, 2)
+                nc.vector.tensor_tensor(
+                    out=up[g][:],
+                    in0=xx[g][:].rearrange("p t n -> p n t"),
+                    in1=p23[:].unsqueeze(1).to_broadcast([P, N, T]),
+                    op=ALU.mult,
+                )
+            g = i + 1
+            if ok(g):
+                hq[g] = (st("hq", [P, N], U32, 3), st("hs", [P, N], U8, 3))
+                quant(hp[g], hq[g][0], hq[g][1])
+            g = i - 1
+            if ok(g):
+                uq[g] = (st("uq", [P, N], U32, 2), st("us", [P, N], U8, 2))
+                quant(up[g], uq[g][0], uq[g][1])
+            if ok(i + 2) and i + 2 > 0:
+                widen(i + 2)
+            g = i + 1
+            if ok(g):
+                xq[g] = (st("xq", [P, N], U32, 4), st("xsc", [P, N], U8, 4))
+                quant(xg[g], xq[g][0], xq[g][1])
+            g = i - 2
+            if ok(g):
+                o = st("o", [P, Q, D], F32, 3)
+                for q in range(Q):
+                    nc.scalar.activation(
+                        out=o[:, q, :].rearrange("p (m t) -> p m t", t=T),
+                        in_=banks[q][:].rearrange("p t m -> p m t"),
+                        func=ACT.Copy,
+                        scale=0.25,
+                    )
+                nc.sync.dma_start(out=o_g[g], in_=o[:])
+            g = i
+            if ok(g):
+                mx(z1, g, 0)
+                tanh(z1, t1, "t1", g)
+            g = i - 1
+            if ok(g):
+                mx(z2, g, 1)

@@ -40,47 +40,64 @@ def tile_antisymmetricssprk2step_t_kernel(tc, h, x_bytes, x_scale, w, win, b, p,
         def kt(nm, shape, dt):
             return keep.tile(shape, dt, name=nm, tag=nm, align_bytes=64)
 
-        ht, xt, xs, hp, xg, hq, xq, h1, t1, xx, up, uq, t2, z1, z2, xb, xp, hps = ({} for j in range(18))
+        ht, xs, hp, xg, hq, xq, h1, t1, xx, up, uq, t2, z1, z2, xb, xp, hps, ob, ot, ss, hh, done = ({} for j in range(22))
+        M2 = ()
+        VQ = ()
 
-        def load(g):
+        def load_x(g):
             xb[g] = st("xb", [P, Q, X], U8, 5)
             nc.sync.dma_start(out=xb[g][:], in_=x_g[g])
-            ht[g] = st("ht", [P, Q, D], BF16, 9)
+
+        def load_h(g):
+            ht[g] = st("ht", [P, Q, D], BF16, 11)
             nc.sync.dma_start(out=ht[g][:], in_=h_g[g])
 
+        w_raw = kt("w_raw", [P, T, D], BF16)
+        win_raw = kt("win_raw", [P, T, D], BF16)
+
+        def load(g):
+            load_x(g)
+            load_h(g)
+            if g == 0:
+                nc.sync.dma_start(out=w_raw[:], in_=w.rearrange("(p j) c -> p j c", j=T))
+                nc.sync.dma_start(out=win_raw[:], in_=win.rearrange("(p j) c -> p j c", j=T))
+
+        warm = kt("warm", [P, 1], F32)
+        nc.vector.memset(warm[:], 0.0)
         ident = kt("ident", [P, P], F32)
         make_identity(nc, ident[:])
         ident_b = kt("ident_b", [P, P], BF16)
         make_identity(nc, ident_b[:])
-        warm = kt("warm", [P, 1], F32)
-        nc.vector.memset(warm[:], 0.0)
-        nc.scalar.activation(out=warm[:], in_=warm[:], func=ACT.Tanh)
 
-        sc = kt("sc", [P, Q, X], F32)
-        nc.scalar.dma_start(out=sc[:, 0, :], in_=x_scale.rearrange("o k -> (o k)").partition_broadcast(P))
+        sc4 = kt("sc4", [P, T], F32)
         pb = kt("pb", [P, 2, 2], BF16)
         rb = kt("rb", [P, T], BF16)
         bb = kt("bb", [P, T], BF16)
+        nc.scalar.dma_start(out=sc4[:], in_=x_scale.rearrange("o (p t) -> p (o t)", t=T))
         nc.scalar.dma_start(out=rb[:], in_=r.rearrange("(p t) -> p t", t=T))
         nc.scalar.dma_start(out=pb[:], in_=p.rearrange("(p u e) -> p u e", u=2, e=2))
         nc.scalar.dma_start(out=bb[:], in_=b.rearrange("(p t) -> p t", t=T))
-
-        w_raw = kt("w_raw", [P, T, D], BF16)
-        win_raw = kt("win_raw", [P, T, D], BF16)
-        xb[0] = st("xb", [P, Q, X], U8, 5)
-        nc.sync.dma_start(out=xb[0][:], in_=x_g[0])
-        nc.sync.dma_start(out=w_raw[:], in_=w.rearrange("(p j) c -> p j c", j=T))
-        ht[0] = st("ht", [P, Q, D], BF16, 9)
-        nc.sync.dma_start(out=ht[0][:], in_=h_g[0])
-        nc.sync.dma_start(out=win_raw[:], in_=win.rearrange("(p j) c -> p j c", j=T))
-        for g in range(1, 4):
-            load(g)
-
-        nc.scalar.copy(out=sc[:, 1, :], in_=sc[:, 0, :])
+        nc.scalar.activation(out=warm[:], in_=warm[:], func=ACT.Tanh)
         two_b = kt("two_b", [P, P], BF16)
+        neg_b = kt("neg_b", [P, P], BF16)
         nc.vector.tensor_scalar(out=two_b[:], in0=ident_b[:], scalar1=2.0, scalar2=None, op0=ALU.mult)
+        nc.vector.tensor_scalar(out=neg_b[:], in0=ident_b[:], scalar1=-1.0, scalar2=None, op0=ALU.mult)
         p23 = kt("p23", [P, T], F32)
-        nc.vector.tensor_scalar(out=p23[:], in0=pb[:].rearrange("p u e -> p (u e)"), scalar1=2.0 / 3.0, scalar2=None, op0=ALU.mult)
+        r4 = kt("r4", [P, T], F32)
+        sc = kt("sc", [P, Q, X], F32)
+
+        def spread_scale():
+            bank = ps.tile([P, T, P], F32, name="z00", tag="z00")
+            for t in range(T):
+                nc.tensor.transpose(bank[:, t, :], sc4[:, t : t + 1].to_broadcast([P, P]), ident[:])
+            for q in range(Q):
+                (nc.vector.tensor_copy, nc.scalar.copy)[q](
+                    out=sc[:, q, :].rearrange("p (m t) -> p m t", t=T), in_=bank[:].rearrange("p t m -> p m t")
+                )
+
+        def small():
+            nc.vector.tensor_scalar(out=p23[:], in0=pb[:].rearrange("p u e -> p (u e)"), scalar1=2.0 / 3.0, scalar2=None, op0=ALU.mult)
+            nc.vector.tensor_copy(out=r4[:], in_=rb[:])
 
         def widen(g):
             xs[g] = st("xs", [P, Q, X], BF16, 3)
@@ -91,41 +108,40 @@ def tile_antisymmetricssprk2step_t_kernel(tc, h, x_bytes, x_scale, w, win, b, p,
                 op=ALU.mult,
             )
 
-        widen(0)
-
-        wdiff = kt("wdiff", [P, T, D], F32)
+        a_pl = kt("a_pl", [P, T, D], BF16)
         a_il = kt("a_il", [P, D, T], BF16)
-        for half in range(2):
-            wt = ps.tile([P, 2, T, P], BF16, name="wt", tag="o%d" % half)
-            for jj in range(2):
-                j = 2 * half + jj
-                for t in range(T):
-                    nc.tensor.transpose(wt[:, jj, t, :], w_raw[:, t, j::T], ident_b[:])
-            for jj in range(2):
-                j = 2 * half + jj
-                nc.vector.tensor_tensor(
-                    out=wdiff[:, j, :].rearrange("p (t m) -> p t m", t=T),
-                    in0=w_raw[:, j, :].rearrange("p (m t) -> p t m", t=T),
-                    in1=wt[:, jj],
-                    op=ALU.subtract,
-                )
-        nc.vector.tensor_tensor(
-            out=a_il[:],
-            in0=wdiff[:].rearrange("p j s -> p s j"),
-            in1=rb[:].unsqueeze(1).to_broadcast([P, D, T]),
-            op=ALU.mult,
-        )
         win_il = kt("win_il", [P, D, T], BF16)
-        for t in range(T):
-            nc.scalar.copy(
-                out=win_il[:, t * P : (t + 1) * P, :],
-                in_=win_raw[:].rearrange("p j (m t) -> p t m j", t=T)[:, t],
-            )
         aq, asc = kt("aq", [P, D], U32), kt("asc", [P, D], U8)
         wq, wsc = kt("wq", [P, D], U32), kt("wsc", [P, D], U8)
 
         def quant(src, codes, scales):
-            nc.vector.quantize_mx(out=codes[:].bitcast(FP8X4), scales=scales[:], in_=src[:].rearrange("p n t -> p (n t)"))
+            nc.vector.quantize_mx(out=codes.bitcast(FP8X4), scales=scales, in_=src.rearrange("p n t -> p (n t)"))
+
+        def diff_w():
+            for j, tag in enumerate(("o0", "o1", "z10", "z11")):
+                bank = ps.tile([P, T, P], F32, name=tag, tag=tag)
+                nc.tensor.matmul(bank[:], ident_b[:], w_raw[:, j, :].rearrange("p (m t) -> p t m", t=T), start=True, stop=False)
+                for t in range(T):
+                    nc.tensor.matmul(bank[:, t, :], w_raw[:, t, j::T], neg_b[:], start=False, stop=t == T - 1)
+                nc.scalar.activation(
+                    out=a_pl[:, j, :], in_=bank[:].rearrange("p t m -> p (t m)"), func=ACT.Copy, scale=r4[:, j : j + 1]
+                )
+
+        def quant_a():
+            nc.vector.tensor_copy(
+                out=a_il[:].rearrange("p (c k) j -> p c j k", k=4), in_=a_pl[:].rearrange("p j (c k) -> p c j k", k=4)
+            )
+            quant(a_il[:], aq[:], asc[:])
+
+        def lay_win():
+            for t in range(T):
+                (nc.vector.tensor_copy if t % 2 else nc.scalar.copy)(
+                    out=win_il[:, t * P : (t + 1) * P, :],
+                    in_=win_raw[:].rearrange("p j (m t) -> p t m j", t=T)[:, t],
+                )
+
+        def quant_win():
+            quant(win_il[:], wq[:], wsc[:])
 
         def turn(tag, src, g):
             words = src[g][:].bitcast(F32)
@@ -135,121 +151,180 @@ def tile_antisymmetricssprk2step_t_kernel(tc, h, x_bytes, x_scale, w, win, b, p,
                     nc.tensor.transpose(bank[:, u, q * P : (q + 1) * P], words[:, q, u::2], ident[:])
             return bank
 
-        def mx(z, g, second):
-            z[g] = []
-            for half in range(2):
-                bank = ps.tile([P, 2, N], F32, name="z%d%d" % (second, half), tag="z%d%d" % (second, half))
-                for tt in range(2):
-                    t = 2 * half + tt
-                    cols = slice(t * P, (t + 1) * P)
-                    m = (uq if second else hq)[g]
-                    for lc, ls, rc, rs, first in ((wq, wsc, xq[g][0], xq[g][1], True), (aq, asc, m[0], m[1], False)):
-                        nc.tensor.matmul_mx(
-                            out=bank[:, tt, :],
-                            lhsT=lc[:, cols].bitcast(FP8X4),
-                            lhsT_scale=ls[:, cols],
-                            rhs=rc[:].bitcast(FP8X4),
-                            rhs_scale=rs[:],
-                            start=first,
-                            stop=not first,
-                        )
-                z[g].append(bank)
+        def turn_h(g):
+            hps[g] = turn("hps", ht, g)
 
-        def tanh(z, dst, nm, g):
-            dst[g] = st(nm, [P, T, N], F32, 3)
-            for t in range(T):
-                nc.scalar.activation(out=dst[g][:, t, :], in_=z[g][t // 2][:, t % 2, :], func=ACT.Tanh, bias=bb[:, t : t + 1])
+        def turn_x(g):
+            xp[g] = turn("xp", xs, g)
 
-        def ok(g):
-            return 0 <= g < NG
+        def gain_h(g):
+            hp[g] = st("hp", [P, N, T], BF16, 2)
+            nc.vector.tensor_tensor(
+                out=hp[g][:].rearrange("p n (u e) -> p n u e", e=2),
+                in0=hps[g][:].bitcast(BF16).rearrange("p u (n e) -> p n u e", e=2),
+                in1=pb[:].unsqueeze(1).to_broadcast([P, N, 2, 2]),
+                op=ALU.mult,
+            )
 
-        for i in range(-2, NG + 2):
-            if ok(i + 4) and i + 4 >= 4:
-                load(i + 4)
-            g = i + 1
-            if ok(g):
-                hps[g] = turn("hps", ht, g)
-                xp[g] = turn("xp", xs, g)
-            g = i - 2
-            if ok(g):
-                tanh(z2, t2, "t2", g)
-            g = i - 1
-            if ok(g):
-                xx[g] = st("xx", [P, T, N], F32, 3)
-                nc.vector.scalar_tensor_tensor(out=xx[g][:], in0=t1[g][:], scalar=0.75, in1=h1[g][:], op0=ALU.mult, op1=ALU.add)
-            g = i + 1
-            if ok(g):
-                pairs = hps[g][:].bitcast(BF16).rearrange("p u (n e) -> p u n e", e=2)
-                hp[g] = st("hp", [P, N, T], BF16, 2)
-                nc.vector.tensor_tensor(
-                    out=hp[g][:].rearrange("p n (u e) -> p n u e", e=2),
-                    in0=pairs.rearrange("p u n e -> p n u e"),
-                    in1=pb[:].unsqueeze(1).to_broadcast([P, N, 2, 2]),
-                    op=ALU.mult,
-                )
-                xg[g] = st("xg", [P, N, T], BF16, 2)
-                nc.scalar.copy(out=xg[g][:].bitcast(F32), in_=xp[g][:].rearrange("p u n -> p n u"))
-                h1[g] = st("h1", [P, T, N], F32, 4)
-                nc.scalar.activation(
-                    out=h1[g][:].rearrange("p (u e) n -> p u e n", e=2),
-                    in_=pairs.rearrange("p u n e -> p u e n"),
-                    func=ACT.Copy,
-                    scale=1.125,
-                )
-            g = i - 2
-            banks = []
-            if ok(g):
-                for q in range(Q):
-                    bank = ps.tile([P, T, P], F32, name="o%d" % q, tag="o%d" % q)
-                    nc.tensor.matmul(bank[:], two_b[:], ht[g][:, q, :].rearrange("p (m t) -> p t m", t=T), start=True, stop=False)
-                    for src in (xx, t2):
-                        for t in range(T):
-                            nc.tensor.matmul(
-                                bank[:, t, :], src[g][:, t, q * P : (q + 1) * P], ident[:],
-                                start=False, stop=(src is t2 and t == T - 1), is_transpose=True,
-                            )
-                    banks.append(bank)
-            if i == -1:
-                quant(a_il, aq, asc)
-                quant(win_il, wq, wsc)
-            g = i - 1
-            if ok(g):
-                up[g] = st("up", [P, N, T], BF16, 2)
-                nc.vector.tensor_tensor(
-                    out=up[g][:],
-                    in0=xx[g][:].rearrange("p t n -> p n t"),
-                    in1=p23[:].unsqueeze(1).to_broadcast([P, N, T]),
-                    op=ALU.mult,
-                )
-            g = i + 1
-            if ok(g):
-                hq[g] = (st("hq", [P, N], U32, 3), st("hs", [P, N], U8, 3))
-                quant(hp[g], hq[g][0], hq[g][1])
-            g = i - 1
-            if ok(g):
-                uq[g] = (st("uq", [P, N], U32, 2), st("us", [P, N], U8, 2))
-                quant(up[g], uq[g][0], uq[g][1])
-            if ok(i + 2) and i + 2 > 0:
-                widen(i + 2)
-            g = i + 1
-            if ok(g):
-                xq[g] = (st("xq", [P, N], U32, 4), st("xsc", [P, N], U8, 4))
-                quant(xg[g], xq[g][0], xq[g][1])
-            g = i - 2
-            if ok(g):
-                o = st("o", [P, Q, D], F32, 3)
-                for q in range(Q):
-                    nc.scalar.activation(
-                        out=o[:, q, :].rearrange("p (m t) -> p m t", t=T),
-                        in_=banks[q][:].rearrange("p t m -> p m t"),
-                        func=ACT.Copy,
-                        scale=0.25,
+        def scale_h(g):
+            h1[g] = st("h1", [P, T, N], F32, 4)
+            nc.scalar.activation(
+                out=h1[g][:].rearrange("p (u e) n -> p u e n", e=2),
+                in_=hps[g][:].bitcast(BF16).rearrange("p u (n e) -> p u e n", e=2),
+                func=ACT.Copy,
+                scale=1.125,
+            )
+
+        def empty_x(g):
+            xg[g] = st("xg", [P, N, T], BF16, 2)
+            nc.scalar.copy(out=xg[g][:].bitcast(F32), in_=xp[g][:].rearrange("p u n -> p n u"))
+
+        def quant_h(g):
+            hq[g] = (st("hq", [P, N], U32, 3), st("hs", [P, N], U8, 3))
+            quant(hp[g][:], hq[g][0][:], hq[g][1][:])
+
+        def quant_x(g):
+            xq[g] = (st("xq", [P, N], U32, 5), st("xsc", [P, N], U8, 5))
+            quant(xg[g][:], xq[g][0][:], xq[g][1][:])
+
+        def mx(nm, g, half, m):
+            tag = "%s%d" % (nm, half)
+            bank = ps.tile([P, 2, N], F32, name=tag, tag=tag)
+            for tt in range(2):
+                t = 2 * half + tt
+                cols = slice(t * P, (t + 1) * P)
+                for lc, ls, rhs, first in ((wq, wsc, xq[g], True), (aq, asc, m[g], False)):
+                    nc.tensor.matmul_mx(
+                        out=bank[:, tt, :],
+                        lhsT=lc[:, cols].bitcast(FP8X4),
+                        lhsT_scale=ls[:, cols],
+                        rhs=rhs[0][:].bitcast(FP8X4),
+                        rhs_scale=rhs[1][:],
+                        start=first,
+                        stop=not first,
                     )
-                nc.sync.dma_start(out=o_g[g], in_=o[:])
-            g = i
-            if ok(g):
-                mx(z1, g, 0)
-                tanh(z1, t1, "t1", g)
-            g = i - 1
-            if ok(g):
-                mx(z2, g, 1)
+            return bank
+
+        def stage1(g, half):
+            z1[g, half] = mx("z0", g, half, hq)
+
+        def stage2(g, half):
+            z2[g, half] = mx("z1", g, half, uq)
+
+        def tanh(dst, z, half):
+            for tt in range(2):
+                t = 2 * half + tt
+                nc.scalar.activation(out=dst[:, t, :], in_=z[:, tt, :], func=ACT.Tanh, bias=bb[:, t : t + 1])
+
+        def tanh1(g, half):
+            if g not in t1:
+                t1[g] = st("t1", [P, T, N], F32, 3)
+            tanh(t1[g], z1[g, half], half)
+
+        def tanh2(g, half):
+            if g not in t2:
+                t2[g] = st("t2", [P, T, N], F32, 4)
+            tanh(t2[g], z2[g, half], half)
+
+        def mix(g):
+            xx[g] = st("xx", [P, T, N], F32, 5)
+            nc.vector.scalar_tensor_tensor(out=xx[g][:], in0=t1[g][:], scalar=0.75, in1=h1[g][:], op0=ALU.mult, op1=ALU.add)
+
+        def gain_u(g):
+            up[g] = st("up", [P, N, T], BF16, 2)
+            nc.vector.tensor_tensor(
+                out=up[g][:].rearrange("p (c k) t -> p c t k", k=4),
+                in0=xx[g][:].rearrange("p t (c k) -> p c t k", k=4),
+                in1=p23[:].unsqueeze(1).unsqueeze(3).to_broadcast([P, N // 4, T, 4]),
+                op=ALU.mult,
+            )
+
+        def quant_u(g):
+            uq[g] = (st("uq", [P, N], U32, 2), st("us", [P, N], U8, 2))
+            quant(up[g][:], uq[g][0][:], uq[g][1][:])
+
+        def add_s(g):
+            if g in M2:
+                ss[g] = st("ss", [P, T, N], F32, 2)
+                nc.vector.tensor_tensor(out=ss[g][:], in0=xx[g][:], in1=t2[g][:], op=ALU.add)
+
+        def sum_out(g, q):
+            bank = ps.tile([P, P // 2, T, 2], F32, name="o%d" % q, tag="o%d" % q)
+            with_h = (g, q) not in VQ
+            if with_h:
+                nc.tensor.matmul(
+                    bank[:], two_b[:], ht[g][:, q, :].rearrange("p (c i t) -> p c t i", i=2, t=T), start=True, stop=False
+                )
+            parts = (ss,) if g in M2 else (xx, t2)
+            for j, src in enumerate(parts):
+                for t in range(T):
+                    nc.tensor.matmul(
+                        bank[:, :, t, :],
+                        src[g][:, t, q * P : (q + 1) * P],
+                        ident[:],
+                        start=(j == 0 and t == 0 and not with_h),
+                        stop=(j == len(parts) - 1 and t == T - 1),
+                        is_transpose=True,
+                    )
+            ob[g, q] = bank
+            if not with_h:
+                hh[g] = st("hh", [P, D], BF16, 3)
+                nc.vector.tensor_scalar(out=hh[g][:], in0=ht[g][:, q, :], scalar1=0.5, scalar2=None, op0=ALU.mult)
+
+        def empty_out(g, q):
+            if g not in ot:
+                ot[g] = st("o", [P, Q, D], F32, 3)
+            dst = ot[g][:, q, :].rearrange("p (c i t) -> p c i t", i=2, t=T)
+            src = ob[g, q][:].rearrange("p c t i -> p c i t")
+            if (g, q) in VQ:
+                nc.vector.scalar_tensor_tensor(
+                    out=ot[g][:, q, :], in0=ob[g, q][:].rearrange("p c t i -> p c i t"), scalar=0.25, in1=hh[g][:], op0=ALU.mult, op1=ALU.add
+                )
+            else:
+                nc.scalar.activation(out=dst, in_=src, func=ACT.Copy, scale=0.25)
+            done[g] = done.get(g, 0) + 1
+            if done[g] == Q:
+                nc.sync.dma_start(out=o_g[g], in_=ot[g][:])
+
+        def weights():
+            diff_w()
+            lay_win()
+            quant_win()
+            quant_a()
+
+        spread_scale()
+        small()
+        order = (
+            (load, -5),
+            (sum_out, 4, 1),
+            (gain_u, 2),
+            (turn_x, -1),
+            (sum_out, 3, 0),
+            (gain_h, -1),
+            (stage1, 0, 0),
+            (scale_h, -1),
+            (quant_u, 2),
+            (stage1, 0, 1),
+            (stage2, 2, 1),
+            (empty_out, 4, 1),
+            (stage2, 2, 0),
+            (empty_out, 3, 0),
+            (widen, -2),
+            (quant_h, -1),
+            (empty_x, -1),
+            (tanh1, 0, 0),
+            (tanh2, 2, 1),
+            (tanh2, 2, 0),
+            (tanh1, 0, 1),
+            (mix, 1),
+            (turn_h, -2),
+            (quant_x, -1),
+        )
+        for i in range(-5, NG + 4):
+            for step, lag, *part in order:
+                g = i - lag
+                if 0 <= g < NG:
+                    if step is stage1 and g == 0 and not done.get("weights"):
+                        done["weights"] = 1
+                        weights()
+                    step(g, *part)

@@ -27,6 +27,7 @@ def tile_antisymmetricssprk2step_t_kernel(tc, h, x_bytes, x_scale, w, win, b, p,
     h_g = h.rearrange("(g p q) d -> g p q d", p=P, q=Q)
     x_g = x_bytes.rearrange("(g p q) d -> g p q d", p=P, q=Q)
     o_g = out.rearrange("(g p q) d -> g p q d", p=P, q=Q)
+    XV, VQ, M2 = set((2, 10, 18)), set(()), set((1, 4, 6, 9, 12, 14, 17, 20, 22))
 
     with ExitStack() as ctx:
         keep = ctx.enter_context(tc.tile_pool(name="keep", bufs=1))
@@ -40,34 +41,30 @@ def tile_antisymmetricssprk2step_t_kernel(tc, h, x_bytes, x_scale, w, win, b, p,
         def kt(nm, shape, dt):
             return keep.tile(shape, dt, name=nm, tag=nm, align_bytes=64)
 
-        ht, xs, hp, xg, hq, xq, h1, t1, xx, up, uq, t2, z1, z2, xb, xp, hps, ob, ot, ss, hh, done = ({} for j in range(22))
-        M2 = ()
-        VQ = ()
+        def bank_of(tag, shape, dt):
+            return ps.tile(shape, dt, name=tag, tag=tag)
 
-        def load_x(g):
-            xb[g] = st("xb", [P, Q, X], U8, 5)
-            nc.sync.dma_start(out=xb[g][:], in_=x_g[g])
-
-        def load_h(g):
-            ht[g] = st("ht", [P, Q, D], BF16, 11)
-            nc.sync.dma_start(out=ht[g][:], in_=h_g[g])
+        ht, xs, hp, xg, hq, xq, h1, t1, xx, up, uq, t2, z1, z2, xb, xp, hps, ob, ot, ss, hh, wt, done = ({} for j in range(23))
 
         w_raw = kt("w_raw", [P, T, D], BF16)
         win_raw = kt("win_raw", [P, T, D], BF16)
 
         def load(g):
-            load_x(g)
-            load_h(g)
             if g == 0:
                 nc.sync.dma_start(out=w_raw[:], in_=w.rearrange("(p j) c -> p j c", j=T))
+            xb[g] = st("xb", [P, Q, X], U8, 6)
+            nc.sync.dma_start(out=xb[g][:], in_=x_g[g])
+            ht[g] = st("ht", [P, Q, D], BF16, 12)
+            nc.sync.dma_start(out=ht[g][:], in_=h_g[g])
+            if g == 0:
                 nc.sync.dma_start(out=win_raw[:], in_=win.rearrange("(p j) c -> p j c", j=T))
 
         warm = kt("warm", [P, 1], F32)
         nc.vector.memset(warm[:], 0.0)
-        ident = kt("ident", [P, P], F32)
-        make_identity(nc, ident[:])
         ident_b = kt("ident_b", [P, P], BF16)
         make_identity(nc, ident_b[:])
+        ident = kt("ident", [P, P], F32)
+        make_identity(nc, ident[:])
 
         sc4 = kt("sc4", [P, T], F32)
         pb = kt("pb", [P, 2, 2], BF16)
@@ -79,25 +76,72 @@ def tile_antisymmetricssprk2step_t_kernel(tc, h, x_bytes, x_scale, w, win, b, p,
         nc.scalar.dma_start(out=bb[:], in_=b.rearrange("(p t) -> p t", t=T))
         nc.scalar.activation(out=warm[:], in_=warm[:], func=ACT.Tanh)
         two_b = kt("two_b", [P, P], BF16)
-        neg_b = kt("neg_b", [P, P], BF16)
         nc.vector.tensor_scalar(out=two_b[:], in0=ident_b[:], scalar1=2.0, scalar2=None, op0=ALU.mult)
+        neg_b = kt("neg_b", [P, P], BF16)
         nc.vector.tensor_scalar(out=neg_b[:], in0=ident_b[:], scalar1=-1.0, scalar2=None, op0=ALU.mult)
         p23 = kt("p23", [P, T], F32)
+        p12 = kt("p12", [P, T], F32)
         r4 = kt("r4", [P, T], F32)
         sc = kt("sc", [P, Q, X], F32)
 
         def spread_scale():
-            bank = ps.tile([P, T, P], F32, name="z00", tag="z00")
+            bank = bank_of("z00", [P, T, P], F32)
             for t in range(T):
                 nc.tensor.transpose(bank[:, t, :], sc4[:, t : t + 1].to_broadcast([P, P]), ident[:])
             for q in range(Q):
                 (nc.vector.tensor_copy, nc.scalar.copy)[q](
                     out=sc[:, q, :].rearrange("p (m t) -> p m t", t=T), in_=bank[:].rearrange("p t m -> p m t")
                 )
-
-        def small():
-            nc.vector.tensor_scalar(out=p23[:], in0=pb[:].rearrange("p u e -> p (u e)"), scalar1=2.0 / 3.0, scalar2=None, op0=ALU.mult)
             nc.vector.tensor_copy(out=r4[:], in_=rb[:])
+            nc.vector.tensor_scalar(out=p12[:], in0=pb[:].rearrange("p u e -> p (u e)"), scalar1=0.5, scalar2=None, op0=ALU.mult)
+            nc.vector.tensor_scalar(out=p23[:], in0=pb[:].rearrange("p u e -> p (u e)"), scalar1=2.0 / 3.0, scalar2=None, op0=ALU.mult)
+
+        def quant(src, codes, scales):
+            nc.vector.quantize_mx(out=codes.bitcast(FP8X4), scales=scales, in_=src.rearrange("p n t -> p (n t)"))
+
+        a_pl = kt("a_pl", [P, T, D], BF16)
+        a_il = kt("a_il", [P, D, T], BF16)
+        win_il = kt("win_il", [P, D, T], BF16)
+        aq, asc = kt("aq", [P, D], U32), kt("asc", [P, D], U8)
+        wq, wsc = kt("wq", [P, D], U32), kt("wsc", [P, D], U8)
+
+        def diff_w(g, half):
+            two = slice(2 * half, 2 * half + 2)
+            for j, tag in enumerate(("o0", "o1", "z10", "z11")):
+                bank = bank_of(tag, [P, 2, P], F32)
+                nc.tensor.matmul(bank[:], ident_b[:], w_raw[:, j, :].rearrange("p (m t) -> p t m", t=T)[:, two, :], start=True, stop=False)
+                for tt in range(2):
+                    nc.tensor.matmul(bank[:, tt, :], w_raw[:, 2 * half + tt, j::T], neg_b[:], start=False, stop=tt == 1)
+                wt[half, j] = bank
+
+        def gain_w(g, half):
+            c = slice(half * D // 2, (half + 1) * D // 2)
+            for j in range(T):
+                nc.scalar.activation(
+                    out=a_pl[:, j, c], in_=wt[half, j][:].rearrange("p t m -> p (t m)"), func=ACT.Copy, scale=r4[:, j : j + 1]
+                )
+
+        def quant_a(g, half):
+            c = slice(half * D // 2, (half + 1) * D // 2)
+            nc.vector.tensor_copy(
+                out=a_il[:, c, :].rearrange("p (c k) j -> p c j k", k=4),
+                in_=a_pl[:, :, c].rearrange("p j (c k) -> p c j k", k=4),
+            )
+            quant(a_il[:, c, :], aq[:, c], asc[:, c])
+
+        def lay_win():
+            for t in range(T):
+                nc.gpsimd.tensor_scalar(
+                    out=win_il[:, t * P : (t + 1) * P, :],
+                    in0=win_raw[:].rearrange("p j (m t) -> p t m j", t=T)[:, t],
+                    scalar1=1.0,
+                    scalar2=0.0,
+                    op0=ALU.mult,
+                    op1=ALU.add,
+                )
+
+        def quant_win(g):
+            quant(win_il[:], wq[:], wsc[:])
 
         def widen(g):
             xs[g] = st("xs", [P, Q, X], BF16, 3)
@@ -108,57 +152,22 @@ def tile_antisymmetricssprk2step_t_kernel(tc, h, x_bytes, x_scale, w, win, b, p,
                 op=ALU.mult,
             )
 
-        a_pl = kt("a_pl", [P, T, D], BF16)
-        a_il = kt("a_il", [P, D, T], BF16)
-        win_il = kt("win_il", [P, D, T], BF16)
-        aq, asc = kt("aq", [P, D], U32), kt("asc", [P, D], U8)
-        wq, wsc = kt("wq", [P, D], U32), kt("wsc", [P, D], U8)
-
-        def quant(src, codes, scales):
-            nc.vector.quantize_mx(out=codes.bitcast(FP8X4), scales=scales, in_=src.rearrange("p n t -> p (n t)"))
-
-        def diff_w():
-            for j, tag in enumerate(("o0", "o1", "z10", "z11")):
-                bank = ps.tile([P, T, P], F32, name=tag, tag=tag)
-                nc.tensor.matmul(bank[:], ident_b[:], w_raw[:, j, :].rearrange("p (m t) -> p t m", t=T), start=True, stop=False)
-                for t in range(T):
-                    nc.tensor.matmul(bank[:, t, :], w_raw[:, t, j::T], neg_b[:], start=False, stop=t == T - 1)
-                nc.scalar.activation(
-                    out=a_pl[:, j, :], in_=bank[:].rearrange("p t m -> p (t m)"), func=ACT.Copy, scale=r4[:, j : j + 1]
-                )
-
-        def quant_a():
-            nc.vector.tensor_copy(
-                out=a_il[:].rearrange("p (c k) j -> p c j k", k=4), in_=a_pl[:].rearrange("p j (c k) -> p c j k", k=4)
-            )
-            quant(a_il[:], aq[:], asc[:])
-
-        def lay_win():
-            for t in range(T):
-                (nc.vector.tensor_copy if t % 2 else nc.scalar.copy)(
-                    out=win_il[:, t * P : (t + 1) * P, :],
-                    in_=win_raw[:].rearrange("p j (m t) -> p t m j", t=T)[:, t],
-                )
-
-        def quant_win():
-            quant(win_il[:], wq[:], wsc[:])
-
-        def turn(tag, src, g):
-            words = src[g][:].bitcast(F32)
-            bank = ps.tile([P, 2, N], F32, name=tag, tag=tag)
+        def turn(tag, src):
+            words = src[:].bitcast(F32)
+            bank = bank_of(tag, [P, 2, N], F32)
             for q in range(Q):
                 for u in range(2):
                     nc.tensor.transpose(bank[:, u, q * P : (q + 1) * P], words[:, q, u::2], ident[:])
             return bank
 
         def turn_h(g):
-            hps[g] = turn("hps", ht, g)
+            hps[g] = turn("hps", ht[g])
 
         def turn_x(g):
-            xp[g] = turn("xp", xs, g)
+            xp[g] = turn("xp", xs[g])
 
         def gain_h(g):
-            hp[g] = st("hp", [P, N, T], BF16, 2)
+            hp[g] = st("hp", [P, N, T], BF16, 3)
             nc.vector.tensor_tensor(
                 out=hp[g][:].rearrange("p n (u e) -> p n u e", e=2),
                 in0=hps[g][:].bitcast(BF16).rearrange("p u (n e) -> p n u e", e=2),
@@ -167,33 +176,36 @@ def tile_antisymmetricssprk2step_t_kernel(tc, h, x_bytes, x_scale, w, win, b, p,
             )
 
         def scale_h(g):
-            h1[g] = st("h1", [P, T, N], F32, 4)
-            nc.scalar.activation(
-                out=h1[g][:].rearrange("p (u e) n -> p u e n", e=2),
-                in_=hps[g][:].bitcast(BF16).rearrange("p u (n e) -> p u e n", e=2),
-                func=ACT.Copy,
-                scale=1.125,
-            )
+            if g in M2:
+                h1[g] = st("h16", [P, N, T], BF16, 4)
+                nc.scalar.copy(out=h1[g][:].bitcast(F32), in_=hps[g][:].rearrange("p u n -> p n u"))
+            else:
+                h1[g] = st("h1", [P, T, N], F32, 4)
+                nc.scalar.activation(
+                    out=h1[g][:].rearrange("p (u e) n -> p u e n", e=2),
+                    in_=hps[g][:].bitcast(BF16).rearrange("p u (n e) -> p u e n", e=2),
+                    func=ACT.Copy,
+                    scale=1.125,
+                )
 
         def empty_x(g):
-            xg[g] = st("xg", [P, N, T], BF16, 2)
-            nc.scalar.copy(out=xg[g][:].bitcast(F32), in_=xp[g][:].rearrange("p u n -> p n u"))
+            xg[g] = st("xg", [P, N, T], BF16, 3)
+            (nc.vector.tensor_copy if g in XV else nc.scalar.copy)(out=xg[g][:].bitcast(F32), in_=xp[g][:].rearrange("p u n -> p n u"))
 
         def quant_h(g):
             hq[g] = (st("hq", [P, N], U32, 3), st("hs", [P, N], U8, 3))
             quant(hp[g][:], hq[g][0][:], hq[g][1][:])
 
         def quant_x(g):
-            xq[g] = (st("xq", [P, N], U32, 5), st("xsc", [P, N], U8, 5))
+            xq[g] = (st("xq", [P, N], U32, 4), st("xsc", [P, N], U8, 4))
             quant(xg[g][:], xq[g][0][:], xq[g][1][:])
 
-        def mx(nm, g, half, m):
-            tag = "%s%d" % (nm, half)
-            bank = ps.tile([P, 2, N], F32, name=tag, tag=tag)
+        def mx(tag, half, xo, mo):
+            bank = bank_of(tag, [P, 2, N], F32)
             for tt in range(2):
                 t = 2 * half + tt
                 cols = slice(t * P, (t + 1) * P)
-                for lc, ls, rhs, first in ((wq, wsc, xq[g], True), (aq, asc, m[g], False)):
+                for lc, ls, rhs, first in ((wq, wsc, xo, True), (aq, asc, mo, False)):
                     nc.tensor.matmul_mx(
                         out=bank[:, tt, :],
                         lhsT=lc[:, cols].bitcast(FP8X4),
@@ -206,125 +218,174 @@ def tile_antisymmetricssprk2step_t_kernel(tc, h, x_bytes, x_scale, w, win, b, p,
             return bank
 
         def stage1(g, half):
-            z1[g, half] = mx("z0", g, half, hq)
+            z1[g, half] = mx("z0%d" % half, half, xq[g], hq[g])
 
         def stage2(g, half):
-            z2[g, half] = mx("z1", g, half, uq)
+            z2[g, half] = mx("z1%d" % half, half, xq[g], uq[g])
 
         def tanh(dst, z, half):
-            for tt in range(2):
+            for tt in (1, 0):
                 t = 2 * half + tt
                 nc.scalar.activation(out=dst[:, t, :], in_=z[:, tt, :], func=ACT.Tanh, bias=bb[:, t : t + 1])
 
         def tanh1(g, half):
             if g not in t1:
-                t1[g] = st("t1", [P, T, N], F32, 3)
+                t1[g] = st("t1", [P, T, N], F32, 2)
             tanh(t1[g], z1[g, half], half)
 
         def tanh2(g, half):
             if g not in t2:
-                t2[g] = st("t2", [P, T, N], F32, 4)
+                t2[g] = st("t2", [P, T, N], F32, 3)
             tanh(t2[g], z2[g, half], half)
 
         def mix(g):
             xx[g] = st("xx", [P, T, N], F32, 5)
-            nc.vector.scalar_tensor_tensor(out=xx[g][:], in0=t1[g][:], scalar=0.75, in1=h1[g][:], op0=ALU.mult, op1=ALU.add)
+            if g in M2:
+                nc.vector.scalar_tensor_tensor(
+                    out=xx[g][:], in0=h1[g][:].rearrange("p n t -> p t n"), scalar=1.5, in1=t1[g][:], op0=ALU.mult, op1=ALU.add
+                )
+            else:
+                nc.vector.scalar_tensor_tensor(out=xx[g][:], in0=t1[g][:], scalar=0.75, in1=h1[g][:], op0=ALU.mult, op1=ALU.add)
 
         def gain_u(g):
             up[g] = st("up", [P, N, T], BF16, 2)
             nc.vector.tensor_tensor(
                 out=up[g][:].rearrange("p (c k) t -> p c t k", k=4),
                 in0=xx[g][:].rearrange("p t (c k) -> p c t k", k=4),
-                in1=p23[:].unsqueeze(1).unsqueeze(3).to_broadcast([P, N // 4, T, 4]),
+                in1=(p12 if g in M2 else p23)[:].unsqueeze(1).unsqueeze(3).to_broadcast([P, N // 4, T, 4]),
                 op=ALU.mult,
             )
 
         def quant_u(g):
+            if g in VQ:
+                hh[g] = st("hh", [P, D], BF16, 3)
+                nc.vector.tensor_scalar(out=hh[g][:], in0=ht[g][:, 1, :], scalar1=0.5, scalar2=None, op0=ALU.mult)
             uq[g] = (st("uq", [P, N], U32, 2), st("us", [P, N], U8, 2))
             quant(up[g][:], uq[g][0][:], uq[g][1][:])
 
         def add_s(g):
             if g in M2:
-                ss[g] = st("ss", [P, T, N], F32, 2)
-                nc.vector.tensor_tensor(out=ss[g][:], in0=xx[g][:], in1=t2[g][:], op=ALU.add)
+                ss[g] = st("ss", [P, T, N], F32, 3)
+                nc.vector.scalar_tensor_tensor(out=ss[g][:], in0=xx[g][:], scalar=0.75, in1=t2[g][:], op0=ALU.mult, op1=ALU.add)
 
         def sum_out(g, q):
-            bank = ps.tile([P, P // 2, T, 2], F32, name="o%d" % q, tag="o%d" % q)
-            with_h = (g, q) not in VQ
-            if with_h:
+            parts = (ss,) if g in M2 else (xx, t2)
+            if g in VQ and q == 1:
+                bank = bank_of("o1", [P, T, P], F32)
+                places = [bank[:, t, :] for t in range(T)]
+                opened = False
+            else:
+                bank = bank_of("o%d" % q, [P, P // 2, T, 2], F32)
+                places = [bank[:, :, t, :] for t in range(T)]
                 nc.tensor.matmul(
                     bank[:], two_b[:], ht[g][:, q, :].rearrange("p (c i t) -> p c t i", i=2, t=T), start=True, stop=False
                 )
-            parts = (ss,) if g in M2 else (xx, t2)
-            for j, src in enumerate(parts):
+                opened = True
+            if opened:
+                for src in parts:
+                    for t in range(T):
+                        nc.tensor.matmul(
+                            places[t], src[g][:, t, q * P : (q + 1) * P], ident[:],
+                            start=False, stop=(src is parts[-1] and t == T - 1), is_transpose=True,
+                        )
+            else:
                 for t in range(T):
-                    nc.tensor.matmul(
-                        bank[:, :, t, :],
-                        src[g][:, t, q * P : (q + 1) * P],
-                        ident[:],
-                        start=(j == 0 and t == 0 and not with_h),
-                        stop=(j == len(parts) - 1 and t == T - 1),
-                        is_transpose=True,
-                    )
+                    for src in parts:
+                        nc.tensor.matmul(
+                            places[t], src[g][:, t, q * P : (q + 1) * P], ident[:],
+                            start=src is parts[0], stop=src is parts[-1], is_transpose=True,
+                        )
             ob[g, q] = bank
-            if not with_h:
-                hh[g] = st("hh", [P, D], BF16, 3)
-                nc.vector.tensor_scalar(out=hh[g][:], in0=ht[g][:, q, :], scalar1=0.5, scalar2=None, op0=ALU.mult)
 
         def empty_out(g, q):
             if g not in ot:
                 ot[g] = st("o", [P, Q, D], F32, 3)
-            dst = ot[g][:, q, :].rearrange("p (c i t) -> p c i t", i=2, t=T)
-            src = ob[g, q][:].rearrange("p c t i -> p c i t")
-            if (g, q) in VQ:
+            if g in VQ and q == 1:
                 nc.vector.scalar_tensor_tensor(
-                    out=ot[g][:, q, :], in0=ob[g, q][:].rearrange("p c t i -> p c i t"), scalar=0.25, in1=hh[g][:], op0=ALU.mult, op1=ALU.add
+                    out=ot[g][:, q, :].rearrange("p (m t) -> p m t", t=T),
+                    in0=ob[g, q][:].rearrange("p t m -> p m t"),
+                    scalar=0.25,
+                    in1=hh[g][:].rearrange("p (m t) -> p m t", t=T),
+                    op0=ALU.mult,
+                    op1=ALU.add,
                 )
             else:
-                nc.scalar.activation(out=dst, in_=src, func=ACT.Copy, scale=0.25)
+                nc.scalar.activation(
+                    out=ot[g][:, q, :].rearrange("p (c i t) -> p c i t", i=2, t=T),
+                    in_=ob[g, q][:].rearrange("p c t i -> p c i t"),
+                    func=ACT.Copy,
+                    scale=0.25,
+                )
             done[g] = done.get(g, 0) + 1
             if done[g] == Q:
                 nc.sync.dma_start(out=o_g[g], in_=ot[g][:])
 
-        def weights():
-            diff_w()
-            lay_win()
-            quant_win()
-            quant_a()
-
-        spread_scale()
-        small()
-        order = (
-            (load, -5),
-            (sum_out, 4, 1),
-            (gain_u, 2),
-            (turn_x, -1),
-            (sum_out, 3, 0),
-            (gain_h, -1),
-            (stage1, 0, 0),
-            (scale_h, -1),
-            (quant_u, 2),
-            (stage1, 0, 1),
-            (stage2, 2, 1),
-            (empty_out, 4, 1),
-            (stage2, 2, 0),
-            (empty_out, 3, 0),
-            (widen, -2),
-            (quant_h, -1),
-            (empty_x, -1),
-            (tanh1, 0, 0),
-            (tanh2, 2, 1),
-            (tanh2, 2, 0),
-            (tanh1, 0, 1),
-            (mix, 1),
-            (turn_h, -2),
-            (quant_x, -1),
+        head = (
+            (diff_w, 0, 0),
+            (gain_w, 0, 0),
+            (widen, 0),
+            (quant_a, 0, 0),
+            (widen, 1),
+            (turn_x, 0),
+            (turn_h, 0),
+            (empty_x, 0),
+            (scale_h, 0),
+            (gain_h, 0),
+            (diff_w, 0, 1),
+            (quant_win, 0),
+            (turn_h, 1),
+            (quant_h, 0),
+            (gain_w, 0, 1),
+            (turn_x, 1),
+            (scale_h, 1),
+            (quant_a, 0, 1),
+            (empty_x, 1),
+            (gain_h, 1),
+            (quant_x, 1),
+            (quant_x, 0),
+            (quant_h, 1),
         )
-        for i in range(-5, NG + 4):
+        order = (
+            (load, -7),
+            (gain_h, -2),
+            (empty_out, 4, 1),
+            (gain_u, 1),
+            (tanh2, 2, 0),
+            (quant_x, -1),
+            (quant_u, 1),
+            (stage1, 0, 1),
+            (turn_x, -2),
+            (stage1, 0, 0),
+            (turn_h, -3),
+            (sum_out, 3, 0),
+            (sum_out, 3, 1),
+            (quant_h, -1),
+            (tanh2, 2, 1),
+            (stage2, 1, 1),
+            (empty_x, -2),
+            (widen, -3),
+            (tanh1, 0, 1),
+            (tanh1, 0, 0),
+            (empty_out, 3, 0),
+            (mix, 0),
+            (add_s, 2),
+            (stage2, 1, 0),
+            (scale_h, -3),
+        )
+        started = set()
+
+        def run(step, g, part):
+            if 0 <= g < NG and (step, g, *part) not in started:
+                started.add((step, g, *part))
+                step(g, *part)
+
+        for g in range(4):
+            run(load, g, [])
+        spread_scale()
+        lay_win()
+        for step, g, *part in head:
+            run(step, g, part)
+        for i in range(-3, NG + 4):
             for step, lag, *part in order:
                 g = i - lag
-                if 0 <= g < NG:
-                    if step is stage1 and g == 0 and not done.get("weights"):
-                        done["weights"] = 1
-                        weights()
-                    step(g, *part)
+                run(step, g, part)

@@ -27,7 +27,7 @@ def tile_antisymmetricssprk2step_t_kernel(tc, h, x_bytes, x_scale, w, win, b, p,
     h_g = h.rearrange("(g p q) d -> g p q d", p=P, q=Q)
     x_g = x_bytes.rearrange("(g p q) d -> g p q d", p=P, q=Q)
     o_g = out.rearrange("(g p q) d -> g p q d", p=P, q=Q)
-    XV, VQ, M2 = set((2, 10, 18)), set(()), set((1, 4, 6, 9, 12, 14, 17, 20, 22))
+    XV, VQ, M2 = set(()), set(()), set(range(1, 24, 2))
 
     with ExitStack() as ctx:
         keep = ctx.enter_context(tc.tile_pool(name="keep", bufs=1))
@@ -144,7 +144,7 @@ def tile_antisymmetricssprk2step_t_kernel(tc, h, x_bytes, x_scale, w, win, b, p,
             quant(win_il[:], wq[:], wsc[:])
 
         def widen(g):
-            xs[g] = st("xs", [P, Q, X], BF16, 3)
+            xs[g] = st("xs", [P, Q, X], BF16, 2)
             nc.vector.tensor_tensor(
                 out=xs[g][:].rearrange("p q k -> p (q k)"),
                 in0=xb[g][:].bitcast(FP8).rearrange("p q k -> p (q k)"),
@@ -189,7 +189,7 @@ def tile_antisymmetricssprk2step_t_kernel(tc, h, x_bytes, x_scale, w, win, b, p,
                 )
 
         def empty_x(g):
-            xg[g] = st("xg", [P, N, T], BF16, 3)
+            xg[g] = st("xg", [P, N, T], BF16, 2)
             (nc.vector.tensor_copy if g in XV else nc.scalar.copy)(out=xg[g][:].bitcast(F32), in_=xp[g][:].rearrange("p u n -> p n u"))
 
         def quant_h(g):
@@ -197,7 +197,7 @@ def tile_antisymmetricssprk2step_t_kernel(tc, h, x_bytes, x_scale, w, win, b, p,
             quant(hp[g][:], hq[g][0][:], hq[g][1][:])
 
         def quant_x(g):
-            xq[g] = (st("xq", [P, N], U32, 4), st("xsc", [P, N], U8, 4))
+            xq[g] = (st("xq", [P, N], U32, 6), st("xsc", [P, N], U8, 6))
             quant(xg[g][:], xq[g][0][:], xq[g][1][:])
 
         def mx(tag, half, xo, mo):
@@ -230,7 +230,7 @@ def tile_antisymmetricssprk2step_t_kernel(tc, h, x_bytes, x_scale, w, win, b, p,
 
         def tanh1(g, half):
             if g not in t1:
-                t1[g] = st("t1", [P, T, N], F32, 2)
+                t1[g] = st("t1", [P, T, N], F32, 3)
             tanh(t1[g], z1[g, half], half)
 
         def tanh2(g, half):
@@ -250,9 +250,9 @@ def tile_antisymmetricssprk2step_t_kernel(tc, h, x_bytes, x_scale, w, win, b, p,
         def gain_u(g):
             up[g] = st("up", [P, N, T], BF16, 2)
             nc.vector.tensor_tensor(
-                out=up[g][:].rearrange("p (c k) t -> p c t k", k=4),
-                in0=xx[g][:].rearrange("p t (c k) -> p c t k", k=4),
-                in1=(p12 if g in M2 else p23)[:].unsqueeze(1).unsqueeze(3).to_broadcast([P, N // 4, T, 4]),
+                out=up[g][:].rearrange("p (c k) t -> p c t k", k=2),
+                in0=xx[g][:].rearrange("p t (c k) -> p c t k", k=2),
+                in1=(p12 if g in M2 else p23)[:].unsqueeze(1).unsqueeze(3).to_broadcast([P, N // 2, T, 2]),
                 op=ALU.mult,
             )
 
@@ -260,12 +260,12 @@ def tile_antisymmetricssprk2step_t_kernel(tc, h, x_bytes, x_scale, w, win, b, p,
             if g in VQ:
                 hh[g] = st("hh", [P, D], BF16, 3)
                 nc.vector.tensor_scalar(out=hh[g][:], in0=ht[g][:, 1, :], scalar1=0.5, scalar2=None, op0=ALU.mult)
-            uq[g] = (st("uq", [P, N], U32, 2), st("us", [P, N], U8, 2))
+            uq[g] = (st("uq", [P, N], U32, 3), st("us", [P, N], U8, 3))
             quant(up[g][:], uq[g][0][:], uq[g][1][:])
 
         def add_s(g):
             if g in M2:
-                ss[g] = st("ss", [P, T, N], F32, 3)
+                ss[g] = st("ss", [P, T, N], F32, 2)
                 nc.vector.scalar_tensor_tensor(out=ss[g][:], in0=xx[g][:], scalar=0.75, in1=t2[g][:], op0=ALU.mult, op1=ALU.add)
 
         def sum_out(g, q):
@@ -321,56 +321,56 @@ def tile_antisymmetricssprk2step_t_kernel(tc, h, x_bytes, x_scale, w, win, b, p,
                 nc.sync.dma_start(out=o_g[g], in_=ot[g][:])
 
         head = (
-            (diff_w, 0, 0),
-            (gain_w, 0, 0),
-            (widen, 0),
-            (quant_a, 0, 0),
-            (widen, 1),
-            (turn_x, 0),
-            (turn_h, 0),
-            (empty_x, 0),
-            (scale_h, 0),
-            (gain_h, 0),
             (diff_w, 0, 1),
-            (quant_win, 0),
-            (turn_h, 1),
-            (quant_h, 0),
+            (widen, 0),
+            (turn_x, 0),
+            (widen, 1),
             (gain_w, 0, 1),
-            (turn_x, 1),
-            (scale_h, 1),
+            (turn_h, 0),
+            (scale_h, 0),
             (quant_a, 0, 1),
-            (empty_x, 1),
+            (gain_h, 0),
+            (diff_w, 0, 0),
+            (turn_h, 1),
+            (quant_win, 0),
             (gain_h, 1),
-            (quant_x, 1),
+            (gain_w, 0, 0),
+            (empty_x, 0),
             (quant_x, 0),
+            (quant_h, 0),
+            (scale_h, 1),
+            (turn_x, 1),
+            (empty_x, 1),
+            (quant_x, 1),
             (quant_h, 1),
+            (quant_a, 0, 0),
         )
         order = (
             (load, -7),
-            (gain_h, -2),
+            (turn_h, -3),
+            (add_s, 3),
+            (stage2, 2, 0),
             (empty_out, 4, 1),
+            (stage1, -1, 0),
+            (widen, -3),
+            (empty_out, 4, 0),
+            (empty_x, -2),
+            (stage1, -1, 1),
+            (scale_h, -3),
+            (sum_out, 3, 1),
+            (tanh2, 2, 1),
+            (tanh1, -1, 0),
             (gain_u, 1),
             (tanh2, 2, 0),
-            (quant_x, -1),
+            (quant_h, -2),
             (quant_u, 1),
-            (stage1, 0, 1),
-            (turn_x, -2),
-            (stage1, 0, 0),
-            (turn_h, -3),
+            (gain_h, -3),
+            (quant_x, -2),
+            (turn_x, -3),
             (sum_out, 3, 0),
-            (sum_out, 3, 1),
-            (quant_h, -1),
-            (tanh2, 2, 1),
-            (stage2, 1, 1),
-            (empty_x, -2),
-            (widen, -3),
-            (tanh1, 0, 1),
-            (tanh1, 0, 0),
-            (empty_out, 3, 0),
             (mix, 0),
-            (add_s, 2),
-            (stage2, 1, 0),
-            (scale_h, -3),
+            (tanh1, -1, 1),
+            (stage2, 1, 1),
         )
         started = set()
 

@@ -44,7 +44,7 @@ def tile_antisymmetricssprk2step_t_kernel(tc, h, x_bytes, x_scale, w, win, b, p,
         def bank_of(tag, shape, dt):
             return ps.tile(shape, dt, name=tag, tag=tag)
 
-        ht, xs, hp, xg, hq, xq, h1, t1, xx, up, uq, t2, z1, z2, xb, xp, hps, ob, ot, ss, hh, wt, done = ({} for j in range(23))
+        ht, xs, hp, xg, hq, xq, h1, t1, xx, up, uq, t2, z1, z2, xb, xp, hps, ob, ot, ss, hh, wt, done, hx = ({} for j in range(24))
 
         w_raw = kt("w_raw", [P, T, D], BF16)
         win_raw = kt("win_raw", [P, T, D], BF16)
@@ -54,7 +54,7 @@ def tile_antisymmetricssprk2step_t_kernel(tc, h, x_bytes, x_scale, w, win, b, p,
                 nc.sync.dma_start(out=w_raw[:], in_=w.rearrange("(p j) c -> p j c", j=T))
             xb[g] = st("xb", [P, Q, X], U8, 6)
             nc.sync.dma_start(out=xb[g][:], in_=x_g[g])
-            ht[g] = st("ht", [P, Q, D], BF16, 12)
+            ht[g] = st("ht", [P, Q, D], BF16, 13)
             nc.sync.dma_start(out=ht[g][:], in_=h_g[g])
             if g == 0:
                 nc.sync.dma_start(out=win_raw[:], in_=win.rearrange("(p j) c -> p j c", j=T))
@@ -144,7 +144,7 @@ def tile_antisymmetricssprk2step_t_kernel(tc, h, x_bytes, x_scale, w, win, b, p,
             quant(win_il[:], wq[:], wsc[:])
 
         def widen(g):
-            xs[g] = st("xs", [P, Q, X], BF16, 2)
+            xs[g] = st("xs", [P, Q, X], BF16, 3)
             nc.vector.tensor_tensor(
                 out=xs[g][:].rearrange("p q k -> p (q k)"),
                 in0=xb[g][:].bitcast(FP8).rearrange("p q k -> p (q k)"),
@@ -166,10 +166,14 @@ def tile_antisymmetricssprk2step_t_kernel(tc, h, x_bytes, x_scale, w, win, b, p,
         def turn_x(g):
             xp[g] = turn("xp", xs[g])
 
+        def both(g):
+            if g not in hx:
+                hx[g] = st("hx", [P, 2, N, T], BF16, 3)
+            return hx[g]
+
         def gain_h(g):
-            hp[g] = st("hp", [P, N, T], BF16, 3)
             nc.vector.tensor_tensor(
-                out=hp[g][:].rearrange("p n (u e) -> p n u e", e=2),
+                out=both(g)[:, 1].rearrange("p n (u e) -> p n u e", e=2),
                 in0=hps[g][:].bitcast(BF16).rearrange("p u (n e) -> p n u e", e=2),
                 in1=pb[:].unsqueeze(1).to_broadcast([P, N, 2, 2]),
                 op=ALU.mult,
@@ -189,16 +193,15 @@ def tile_antisymmetricssprk2step_t_kernel(tc, h, x_bytes, x_scale, w, win, b, p,
                 )
 
         def empty_x(g):
-            xg[g] = st("xg", [P, N, T], BF16, 2)
-            (nc.vector.tensor_copy if g in XV else nc.scalar.copy)(out=xg[g][:].bitcast(F32), in_=xp[g][:].rearrange("p u n -> p n u"))
+            (nc.vector.tensor_copy if g in XV else nc.scalar.copy)(
+                out=both(g)[:, 0].bitcast(F32), in_=xp[g][:].rearrange("p u n -> p n u")
+            )
 
-        def quant_h(g):
-            hq[g] = (st("hq", [P, N], U32, 3), st("hs", [P, N], U8, 3))
-            quant(hp[g][:], hq[g][0][:], hq[g][1][:])
-
-        def quant_x(g):
-            xq[g] = (st("xq", [P, N], U32, 6), st("xsc", [P, N], U8, 6))
-            quant(xg[g][:], xq[g][0][:], xq[g][1][:])
+        def quant_in(g):
+            codes, scales = st("hxq", [P, 2, N], U32, 6), st("hxs", [P, 2, N], U8, 6)
+            quant(hx[g][:].rearrange("p s n t -> p (s n) t"), codes[:].rearrange("p s n -> p (s n)"), scales[:].rearrange("p s n -> p (s n)"))
+            xq[g] = (codes[:, 0], scales[:, 0])
+            hq[g] = (codes[:, 1], scales[:, 1])
 
         def mx(tag, half, xo, mo):
             bank = bank_of(tag, [P, 2, N], F32)
@@ -210,8 +213,8 @@ def tile_antisymmetricssprk2step_t_kernel(tc, h, x_bytes, x_scale, w, win, b, p,
                         out=bank[:, tt, :],
                         lhsT=lc[:, cols].bitcast(FP8X4),
                         lhsT_scale=ls[:, cols],
-                        rhs=rhs[0][:].bitcast(FP8X4),
-                        rhs_scale=rhs[1][:],
+                        rhs=rhs[0].bitcast(FP8X4),
+                        rhs_scale=rhs[1],
                         start=first,
                         stop=not first,
                     )
@@ -230,7 +233,7 @@ def tile_antisymmetricssprk2step_t_kernel(tc, h, x_bytes, x_scale, w, win, b, p,
 
         def tanh1(g, half):
             if g not in t1:
-                t1[g] = st("t1", [P, T, N], F32, 3)
+                t1[g] = st("t1", [P, T, N], F32, 2)
             tanh(t1[g], z1[g, half], half)
 
         def tanh2(g, half):
@@ -260,8 +263,9 @@ def tile_antisymmetricssprk2step_t_kernel(tc, h, x_bytes, x_scale, w, win, b, p,
             if g in VQ:
                 hh[g] = st("hh", [P, D], BF16, 3)
                 nc.vector.tensor_scalar(out=hh[g][:], in0=ht[g][:, 1, :], scalar1=0.5, scalar2=None, op0=ALU.mult)
-            uq[g] = (st("uq", [P, N], U32, 3), st("us", [P, N], U8, 3))
-            quant(up[g][:], uq[g][0][:], uq[g][1][:])
+            codes, scales = st("uq", [P, N], U32, 3), st("us", [P, N], U8, 3)
+            quant(up[g][:], codes[:], scales[:])
+            uq[g] = (codes[:], scales[:])
 
         def add_s(g):
             if g in M2:
@@ -317,60 +321,59 @@ def tile_antisymmetricssprk2step_t_kernel(tc, h, x_bytes, x_scale, w, win, b, p,
                     scale=0.25,
                 )
             done[g] = done.get(g, 0) + 1
-            if done[g] == Q:
+            if g == NG - 1:
+                nc.sync.dma_start(out=o_g[g][:, q, :], in_=ot[g][:, q, :])
+            elif done[g] == Q:
                 nc.sync.dma_start(out=o_g[g], in_=ot[g][:])
 
         head = (
             (diff_w, 0, 1),
             (widen, 0),
-            (turn_x, 0),
             (widen, 1),
-            (gain_w, 0, 1),
             (turn_h, 0),
-            (scale_h, 0),
-            (quant_a, 0, 1),
             (gain_h, 0),
+            (turn_x, 0),
+            (gain_w, 0, 1),
+            (empty_x, 0),
+            (quant_a, 0, 1),
             (diff_w, 0, 0),
-            (turn_h, 1),
+            (turn_x, 1),
+            (scale_h, 0),
             (quant_win, 0),
+            (turn_h, 1),
+            (quant_in, 0),
             (gain_h, 1),
             (gain_w, 0, 0),
-            (empty_x, 0),
-            (quant_x, 0),
-            (quant_h, 0),
-            (scale_h, 1),
-            (turn_x, 1),
-            (empty_x, 1),
-            (quant_x, 1),
-            (quant_h, 1),
             (quant_a, 0, 0),
+            (empty_x, 1),
+            (scale_h, 1),
+            (quant_in, 1),
         )
         order = (
-            (load, -7),
-            (turn_h, -3),
-            (add_s, 3),
-            (stage2, 2, 0),
+            (load, -8),
             (empty_out, 4, 1),
-            (stage1, -1, 0),
-            (widen, -3),
-            (empty_out, 4, 0),
-            (empty_x, -2),
-            (stage1, -1, 1),
-            (scale_h, -3),
-            (sum_out, 3, 1),
-            (tanh2, 2, 1),
-            (tanh1, -1, 0),
+            (stage1, 0, 1),
+            (add_s, 3),
+            (tanh1, 0, 0),
             (gain_u, 1),
-            (tanh2, 2, 0),
-            (quant_h, -2),
+            (stage2, 2, 1),
+            (stage2, 2, 0),
+            (widen, -4),
+            (tanh1, 0, 1),
+            (empty_x, -2),
+            (empty_out, 4, 0),
+            (stage1, -1, 0),
+            (tanh2, 2, 1),
+            (sum_out, 3, 1),
+            (quant_in, -2),
+            (turn_h, -3),
             (quant_u, 1),
-            (gain_h, -3),
-            (quant_x, -2),
-            (turn_x, -3),
-            (sum_out, 3, 0),
             (mix, 0),
-            (tanh1, -1, 1),
-            (stage2, 1, 1),
+            (turn_x, -3),
+            (tanh2, 2, 0),
+            (sum_out, 3, 0),
+            (scale_h, -3),
+            (gain_h, -3),
         )
         started = set()
 
@@ -385,7 +388,7 @@ def tile_antisymmetricssprk2step_t_kernel(tc, h, x_bytes, x_scale, w, win, b, p,
         lay_win()
         for step, g, *part in head:
             run(step, g, part)
-        for i in range(-3, NG + 4):
+        for i in range(-4, NG + 4):
             for step, lag, *part in order:
                 g = i - lag
                 run(step, g, part)

from contextlib import ExitStack

import concourse.mybir as mybir
from concourse.masks import make_identity

F32 = mybir.dt.float32
BF16 = mybir.dt.bfloat16
U32 = mybir.dt.uint32
U8 = mybir.dt.uint8
FP8 = mybir.dt.float8_e4m3fn
FP8X4 = mybir.dt.float8_e4m3fn_x4
ACT = mybir.ActivationFunctionType
ALU = mybir.AluOpType

B, D, X = 6144, 512, 512
P = 128
N = 256
Q = N // P
T = 4
NG = B // N

FLOPS = 3 * 2 * B * D * D


def tile_antisymmetricssprk2step_t_kernel(tc, h, x_bytes, x_scale, w, win, b, p, r, out):
    nc = tc.nc
    h_g = h.rearrange("(g p q) d -> g p q d", p=P, q=Q)
    x_g = x_bytes.rearrange("(g p q) d -> g p q d", p=P, q=Q)
    o_g = out.rearrange("(g p q) d -> g p q d", p=P, q=Q)
    XV, VQ, M2 = set(()), set(()), set(range(1, 24, 2))

    with ExitStack() as ctx:
        keep = ctx.enter_context(tc.tile_pool(name="keep", bufs=1))
        sb = ctx.enter_context(tc.tile_pool(name="sb", bufs=2))
        ps = ctx.enter_context(tc.psum_pool(name="ps", bufs=1))
        ctx.enter_context(tc.manual_schedule())

        def st(nm, shape, dt, bufs):
            return sb.tile(shape, dt, name=nm, tag=nm, bufs=bufs, align_bytes=64)

        def kt(nm, shape, dt):
            return keep.tile(shape, dt, name=nm, tag=nm, align_bytes=64)

        def bank_of(tag, shape, dt):
            return ps.tile(shape, dt, name=tag, tag=tag)

        ht, xs, hp, xg, hq, xq, h1, t1, xx, up, uq, t2, z1, z2, xb, xp, hps, ob, ot, ss, hh, wt, done, hx = ({} for j in range(24))

        w_raw = kt("w_raw", [P, T, D], BF16)
        win_raw = kt("win_raw", [P, T, D], BF16)

        def load(g):
            if g == 0:
                nc.sync.dma_start(out=w_raw[:], in_=w.rearrange("(p j) c -> p j c", j=T))
            xb[g] = st("xb", [P, Q, X], U8, 6)
            nc.sync.dma_start(out=xb[g][:], in_=x_g[g])
            ht[g] = st("ht", [P, Q, D], BF16, 13)
            nc.sync.dma_start(out=ht[g][:], in_=h_g[g])
            if g == 0:
                nc.sync.dma_start(out=win_raw[:], in_=win.rearrange("(p j) c -> p j c", j=T))

        warm = kt("warm", [P, 1], F32)
        nc.vector.memset(warm[:], 0.0)
        ident_b = kt("ident_b", [P, P], BF16)
        make_identity(nc, ident_b[:])
        ident = kt("ident", [P, P], F32)
        make_identity(nc, ident[:])

        sc4 = kt("sc4", [P, T], F32)
        pb = kt("pb", [P, 2, 2], BF16)
        rb = kt("rb", [P, T], BF16)
        bb = kt("bb", [P, T], BF16)
        nc.scalar.dma_start(out=sc4[:], in_=x_scale.rearrange("o (p t) -> p (o t)", t=T))
        nc.scalar.dma_start(out=rb[:], in_=r.rearrange("(p t) -> p t", t=T))
        nc.scalar.dma_start(out=pb[:], in_=p.rearrange("(p u e) -> p u e", u=2, e=2))
        nc.scalar.dma_start(out=bb[:], in_=b.rearrange("(p t) -> p t", t=T))
        nc.scalar.activation(out=warm[:], in_=warm[:], func=ACT.Tanh)
        two_b = kt("two_b", [P, P], BF16)
        nc.vector.tensor_scalar(out=two_b[:], in0=ident_b[:], scalar1=2.0, scalar2=None, op0=ALU.mult)
        neg_b = kt("neg_b", [P, P], BF16)
        nc.vector.tensor_scalar(out=neg_b[:], in0=ident_b[:], scalar1=-1.0, scalar2=None, op0=ALU.mult)
        p23 = kt("p23", [P, T], F32)
        p12 = kt("p12", [P, T], F32)
        r4 = kt("r4", [P, T], F32)
        sc = kt("sc", [P, Q, X], F32)

        def spread_scale():
            bank = bank_of("z00", [P, T, P], F32)
            for t in range(T):
                nc.tensor.transpose(bank[:, t, :], sc4[:, t : t + 1].to_broadcast([P, P]), ident[:])
            for q in range(Q):
                (nc.vector.tensor_copy, nc.scalar.copy)[q](
                    out=sc[:, q, :].rearrange("p (m t) -> p m t", t=T), in_=bank[:].rearrange("p t m -> p m t")
                )
            nc.vector.tensor_copy(out=r4[:], in_=rb[:])
            nc.vector.tensor_scalar(out=p12[:], in0=pb[:].rearrange("p u e -> p (u e)"), scalar1=0.5, scalar2=None, op0=ALU.mult)
            nc.vector.tensor_scalar(out=p23[:], in0=pb[:].rearrange("p u e -> p (u e)"), scalar1=2.0 / 3.0, scalar2=None, op0=ALU.mult)

        def quant(src, codes, scales):
            nc.vector.quantize_mx(out=codes.bitcast(FP8X4), scales=scales, in_=src.rearrange("p n t -> p (n t)"))

        a_pl = kt("a_pl", [P, T, D], BF16)
        a_il = kt("a_il", [P, D, T], BF16)
        win_il = kt("win_il", [P, D, T], BF16)
        aq, asc = kt("aq", [P, D], U32), kt("asc", [P, D], U8)
        wq, wsc = kt("wq", [P, D], U32), kt("wsc", [P, D], U8)

        def diff_w(g, half):
            two = slice(2 * half, 2 * half + 2)
            for j, tag in enumerate(("o0", "o1", "z10", "z11")):
                bank = bank_of(tag, [P, 2, P], F32)
                nc.tensor.matmul(bank[:], ident_b[:], w_raw[:, j, :].rearrange("p (m t) -> p t m", t=T)[:, two, :], start=True, stop=False)
                for tt in range(2):
                    nc.tensor.matmul(bank[:, tt, :], w_raw[:, 2 * half + tt, j::T], neg_b[:], start=False, stop=tt == 1)
                wt[half, j] = bank

        def gain_w(g, half):
            c = slice(half * D // 2, (half + 1) * D // 2)
            for j in range(T):
                nc.scalar.activation(
                    out=a_pl[:, j, c], in_=wt[half, j][:].rearrange("p t m -> p (t m)"), func=ACT.Copy, scale=r4[:, j : j + 1]
                )

        def quant_a(g, half):
            c = slice(half * D // 2, (half + 1) * D // 2)
            nc.vector.tensor_copy(
                out=a_il[:, c, :].rearrange("p (c k) j -> p c j k", k=4),
                in_=a_pl[:, :, c].rearrange("p j (c k) -> p c j k", k=4),
            )
            quant(a_il[:, c, :], aq[:, c], asc[:, c])

        def lay_win():
            for t in range(T):
                nc.gpsimd.tensor_scalar(
                    out=win_il[:, t * P : (t + 1) * P, :],
                    in0=win_raw[:].rearrange("p j (m t) -> p t m j", t=T)[:, t],
                    scalar1=1.0,
                    scalar2=0.0,
                    op0=ALU.mult,
                    op1=ALU.add,
                )

        def quant_win(g):
            quant(win_il[:], wq[:], wsc[:])

        def widen(g):
            xs[g] = st("xs", [P, Q, X], BF16, 3)
            nc.vector.tensor_tensor(
                out=xs[g][:].rearrange("p q k -> p (q k)"),
                in0=xb[g][:].bitcast(FP8).rearrange("p q k -> p (q k)"),
                in1=sc[:].rearrange("p q k -> p (q k)"),
                op=ALU.mult,
            )

        def turn(tag, src):
            words = src[:].bitcast(F32)
            bank = bank_of(tag, [P, 2, N], F32)
            for q in range(Q):
                for u in range(2):
                    nc.tensor.transpose(bank[:, u, q * P : (q + 1) * P], words[:, q, u::2], ident[:])
            return bank

        def turn_h(g):
            hps[g] = turn("hps", ht[g])

        def turn_x(g):
            xp[g] = turn("xp", xs[g])

        def both(g):
            if g not in hx:
                hx[g] = st("hx", [P, 2, N, T], BF16, 3)
            return hx[g]

        def gain_h(g):
            nc.vector.tensor_tensor(
                out=both(g)[:, 1].rearrange("p n (u e) -> p n u e", e=2),
                in0=hps[g][:].bitcast(BF16).rearrange("p u (n e) -> p n u e", e=2),
                in1=pb[:].unsqueeze(1).to_broadcast([P, N, 2, 2]),
                op=ALU.mult,
            )

        def scale_h(g):
            if g in M2:
                h1[g] = st("h16", [P, N, T], BF16, 4)
                nc.scalar.copy(out=h1[g][:].bitcast(F32), in_=hps[g][:].rearrange("p u n -> p n u"))
            else:
                h1[g] = st("h1", [P, T, N], F32, 4)
                nc.scalar.activation(
                    out=h1[g][:].rearrange("p (u e) n -> p u e n", e=2),
                    in_=hps[g][:].bitcast(BF16).rearrange("p u (n e) -> p u e n", e=2),
                    func=ACT.Copy,
                    scale=1.125,
                )

        def empty_x(g):
            (nc.vector.tensor_copy if g in XV else nc.scalar.copy)(
                out=both(g)[:, 0].bitcast(F32), in_=xp[g][:].rearrange("p u n -> p n u")
            )

        def quant_in(g):
            codes, scales = st("hxq", [P, 2, N], U32, 6), st("hxs", [P, 2, N], U8, 6)
            quant(hx[g][:].rearrange("p s n t -> p (s n) t"), codes[:].rearrange("p s n -> p (s n)"), scales[:].rearrange("p s n -> p (s n)"))
            xq[g] = (codes[:, 0], scales[:, 0])
            hq[g] = (codes[:, 1], scales[:, 1])

        def mx(tag, half, xo, mo):
            bank = bank_of(tag, [P, 2, N], F32)
            for tt in range(2):
                t = 2 * half + tt
                cols = slice(t * P, (t + 1) * P)
                for lc, ls, rhs, first in ((wq, wsc, xo, True), (aq, asc, mo, False)):
                    nc.tensor.matmul_mx(
                        out=bank[:, tt, :],
                        lhsT=lc[:, cols].bitcast(FP8X4),
                        lhsT_scale=ls[:, cols],
                        rhs=rhs[0].bitcast(FP8X4),
                        rhs_scale=rhs[1],
                        start=first,
                        stop=not first,
                    )
            return bank

        def stage1(g, half):
            z1[g, half] = mx("z0%d" % half, half, xq[g], hq[g])

        def stage2(g, half):
            z2[g, half] = mx("z1%d" % half, half, xq[g], uq[g])

        def tanh(dst, z, half):
            for tt in (1, 0):
                t = 2 * half + tt
                nc.scalar.activation(out=dst[:, t, :], in_=z[:, tt, :], func=ACT.Tanh, bias=bb[:, t : t + 1])

        def tanh1(g, half):
            if g not in t1:
                t1[g] = st("t1", [P, T, N], F32, 2)
            tanh(t1[g], z1[g, half], half)

        def tanh2(g, half):
            if g not in t2:
                t2[g] = st("t2", [P, T, N], F32, 3)
            tanh(t2[g], z2[g, half], half)

        def mix(g):
            xx[g] = st("xx", [P, T, N], F32, 5)
            if g in M2:
                nc.vector.scalar_tensor_tensor(
                    out=xx[g][:], in0=h1[g][:].rearrange("p n t -> p t n"), scalar=1.5, in1=t1[g][:], op0=ALU.mult, op1=ALU.add
                )
            else:
                nc.vector.scalar_tensor_tensor(out=xx[g][:], in0=t1[g][:], scalar=0.75, in1=h1[g][:], op0=ALU.mult, op1=ALU.add)

        def gain_u(g):
            up[g] = st("up", [P, N, T], BF16, 2)
            nc.vector.tensor_tensor(
                out=up[g][:].rearrange("p (c k) t -> p c t k", k=2),
                in0=xx[g][:].rearrange("p t (c k) -> p c t k", k=2),
                in1=(p12 if g in M2 else p23)[:].unsqueeze(1).unsqueeze(3).to_broadcast([P, N // 2, T, 2]),
                op=ALU.mult,
            )

        def quant_u(g):
            if g in VQ:
                hh[g] = st("hh", [P, D], BF16, 3)
                nc.vector.tensor_scalar(out=hh[g][:], in0=ht[g][:, 1, :], scalar1=0.5, scalar2=None, op0=ALU.mult)
            codes, scales = st("uq", [P, N], U32, 3), st("us", [P, N], U8, 3)
            quant(up[g][:], codes[:], scales[:])
            uq[g] = (codes[:], scales[:])

        def add_s(g):
            if g in M2:
                ss[g] = st("ss", [P, T, N], F32, 2)
                nc.vector.scalar_tensor_tensor(out=ss[g][:], in0=xx[g][:], scalar=0.75, in1=t2[g][:], op0=ALU.mult, op1=ALU.add)

        def sum_out(g, q):
            parts = (ss,) if g in M2 else (xx, t2)
            if g in VQ and q == 1:
                bank = bank_of("o1", [P, T, P], F32)
                places = [bank[:, t, :] for t in range(T)]
                opened = False
            else:
                bank = bank_of("o%d" % q, [P, P // 2, T, 2], F32)
                places = [bank[:, :, t, :] for t in range(T)]
                nc.tensor.matmul(
                    bank[:], two_b[:], ht[g][:, q, :].rearrange("p (c i t) -> p c t i", i=2, t=T), start=True, stop=False
                )
                opened = True
            if opened:
                for src in parts:
                    for t in range(T):
                        nc.tensor.matmul(
                            places[t], src[g][:, t, q * P : (q + 1) * P], ident[:],
                            start=False, stop=(src is parts[-1] and t == T - 1), is_transpose=True,
                        )
            else:
                for t in range(T):
                    for src in parts:
                        nc.tensor.matmul(
                            places[t], src[g][:, t, q * P : (q + 1) * P], ident[:],
                            start=src is parts[0], stop=src is parts[-1], is_transpose=True,
                        )
            ob[g, q] = bank

        def empty_out(g, q):
            if g not in ot:
                ot[g] = st("o", [P, Q, D], F32, 3)
            if g in VQ and q == 1:
                nc.vector.scalar_tensor_tensor(
                    out=ot[g][:, q, :].rearrange("p (m t) -> p m t", t=T),
                    in0=ob[g, q][:].rearrange("p t m -> p m t"),
                    scalar=0.25,
                    in1=hh[g][:].rearrange("p (m t) -> p m t", t=T),
                    op0=ALU.mult,
                    op1=ALU.add,
                )
            else:
                nc.scalar.activation(
                    out=ot[g][:, q, :].rearrange("p (c i t) -> p c i t", i=2, t=T),
                    in_=ob[g, q][:].rearrange("p c t i -> p c i t"),
                    func=ACT.Copy,
                    scale=0.25,
                )
            done[g] = done.get(g, 0) + 1
            if g == NG - 1:
                nc.sync.dma_start(out=o_g[g][:, q, :], in_=ot[g][:, q, :])
            elif done[g] == Q:
                nc.sync.dma_start(out=o_g[g], in_=ot[g][:])

        head = (
            (diff_w, 0, 1),
            (widen, 0),
            (widen, 1),
            (turn_h, 0),
            (gain_h, 0),
            (turn_x, 0),
            (gain_w, 0, 1),
            (empty_x, 0),
            (quant_a, 0, 1),
            (diff_w, 0, 0),
            (turn_x, 1),
            (scale_h, 0),
            (quant_win, 0),
            (turn_h, 1),
            (quant_in, 0),
            (gain_h, 1),
            (gain_w, 0, 0),
            (quant_a, 0, 0),
            (empty_x, 1),
            (scale_h, 1),
            (quant_in, 1),
        )
        order = (
            (load, -8),
            (empty_out, 4, 1),
            (stage1, 0, 1),
            (add_s, 3),
            (tanh1, 0, 0),
            (gain_u, 1),
            (stage2, 2, 1),
            (stage2, 2, 0),
            (widen, -4),
            (tanh1, 0, 1),
            (empty_x, -2),
            (empty_out, 4, 0),
            (stage1, -1, 0),
            (tanh2, 2, 1),
            (sum_out, 3, 1),
            (quant_in, -2),
            (turn_h, -3),
            (quant_u, 1),
            (mix, 0),
            (turn_x, -3),
            (tanh2, 2, 0),
            (sum_out, 3, 0),
            (scale_h, -3),
            (gain_h, -3),
        )
        started = set()

        def run(step, g, part):
            if 0 <= g < NG and (step, g, *part) not in started:
                started.add((step, g, *part))
                step(g, *part)

        for g in range(4):
            run(load, g, [])
        spread_scale()
        lay_win()
        for step, g, *part in head:
            run(step, g, part)
        for i in range(-4, NG + 4):
            for step, lag, *part in order:
                g = i - lag
                run(step, g, part)
